import numpy as np
import ml_dtypes


def mxq(x, axis, fmt="e4m3"):
    dtype, down = {"e4m3": (ml_dtypes.float8_e4m3fn, 7), "e5m2": (ml_dtypes.float8_e5m2, 14)}[fmt]
    v = np.moveaxis(np.asarray(x, np.float32).astype(ml_dtypes.bfloat16).astype(np.float64), axis, -1)
    blocks = v.reshape(v.shape[:-1] + (-1, 32))
    amax = np.abs(blocks).max(-1, keepdims=True)
    byte = np.maximum(np.where(amax > 0, np.frexp(amax)[1] - 1 + 127, 0) - down, 1)
    scale = np.exp2(byte - 127.0)
    codes = (blocks / scale).astype(np.float32).astype(dtype).astype(np.float64)
    return np.moveaxis((codes * scale).reshape(v.shape), -1, axis)


WIDE = False


def mx_kscale(k):
    if not WIDE:
        return np.ones(k)
    levels = np.array([10, -10, 5, -5, 0])
    if k % 512:
        return np.exp2(np.random.permutation(np.resize(levels, k // 32))).repeat(32)
    a = np.empty((k // 512, 16))
    for p in range(k // 512):
        a[p, :8] = np.random.permutation(np.resize(levels, 8))
        for g in range(8):
            far = levels[np.abs(levels - a[p, g]) >= 10]
            a[p, g + 8] = far[np.random.randint(len(far))]
    return np.exp2(a.ravel()).repeat(32)


def f64(x):
    return np.asarray(x).astype(np.float64)


def striped(idx):
    return np.tile(np.asarray(idx).reshape(-1, 16).T, (8, 1)).astype(np.uint16)


def unstriped(offs):
    return offs[:16].T.reshape(-1).astype(np.int64)


E2M1 = np.array([0.0, 0.5, 1.0, 1.5, 2.0, 3.0, 4.0, 6.0, -0.0, -0.5, -1.0, -1.5, -2.0, -3.0, -4.0, -6.0])


def pack_weight(w, fmt):
    k, n = w.shape
    w = f64(np.asarray(w, np.float32).astype(ml_dtypes.bfloat16)).reshape(k // 32, 32, n)
    amax = np.abs(w).max(1)
    if fmt == "e4m3":
        byte = np.frexp(amax)[1] - 1 + 127 - 7
    else:
        mant, ex = np.frexp(amax / 6.0)
        byte = np.where(mant > 0.5, ex, ex - 1) + 127
    byte = np.clip(np.where(amax > 0, byte, 1), 1, 254)
    scaled = (w * np.exp2(127.0 - byte)[:, None, :]).reshape(k, n).astype(np.float32)
    by_word = np.ascontiguousarray(scaled.reshape(k // 512, 128, 4, n).transpose(0, 1, 3, 2))
    if fmt == "e4m3":
        words = by_word.astype(ml_dtypes.float8_e4m3fn).view(np.uint8)
    else:
        c = by_word.astype(ml_dtypes.float4_e2m1fn).view(np.uint8) & 0xF
        words = (c[..., 0::2] | (c[..., 1::2] << 4)).reshape(k // 512, 128, 2 * n)
    return np.ascontiguousarray(words), np.ascontiguousarray(byte.astype(np.uint8).reshape(k // 512, 16, n))


def unpack_weight(words, scales, fmt):
    g, _, n = scales.shape
    words = np.ascontiguousarray(words).reshape(g, 128, n, -1)
    if fmt == "e4m3":
        vals = words.view(ml_dtypes.float8_e4m3fn).astype(np.float64)
    else:
        nib = np.empty((g, 128, n, 4), np.uint8)
        nib[..., 0::2] = words & 0xF
        nib[..., 1::2] = words >> 4
        vals = E2M1[nib]
    vals = vals * np.repeat(np.exp2(scales.astype(np.float64) - 127.0), 8, axis=1)[..., None]
    return vals.transpose(0, 1, 3, 2).reshape(g * 512, n)


D, E, T, I, Q = 512, 512, 2048, 512, 128


def setup_inputs():
    n = np.random.standard_normal
    idx = np.random.permutation(T)[:I]
    fd = mx_kscale(D)
    fe = mx_kscale(E)
    keysp = pack_weight(n((D, T)) / fd[:, None], "e4m3")
    valsp = pack_weight(n((E, T)) / fe[:, None], "e4m3")
    return {
        "query": (n((D, Q)) * 1.0 / np.sqrt(D) * fd[:, None]).astype(np.float32),
        "keys_words": keysp[0],
        "keys_scales": keysp[1],
        "floor": (np.random.uniform(0.05, 0.3, (Q, 1))).astype(np.float32),
        "reserve": (np.random.uniform(20.0, 100.0, (Q, 1))).astype(np.float32),
        "gout": (n((E, Q)) * 1 / np.sqrt(E) * fe[:, None]).astype(np.float32),
        "vals_words": valsp[0],
        "vals_scales": valsp[1],
        "old": (0.5 * n((Q, T))).astype(np.float32),
        "offs": striped(idx),
    }


def reference(query, keys_words, keys_scales, floor, reserve, gout, vals_words, vals_scales, old, offs):
    idx = unstriped(offs)
    keysu = unpack_weight(keys_words, keys_scales, "e4m3")
    valsu = unpack_weight(vals_words, vals_scales, "e4m3")
    queryq = mxq(f64(query), 0, "e4m3")
    keysidxg = keysu[:, idx]
    a = queryq.T @ keysidxg
    p = np.square(a) + f64(floor)
    z = np.sum(p, axis=1, keepdims=True) + f64(reserve)
    goutq = mxq(f64(gout), 0, "e4m3")
    valsidxg = valsu[:, idx]
    c0 = goutq.T @ valsidxg
    dz = np.sum(c0 * p / np.square(z) * (-1.0), axis=1, keepdims=True)
    dp = c0 / z + dz
    da = dp * a * 2.0
    gs = da * 512.0
    gf = np.zeros((Q, T))
    gf[:, idx] = gs
    y = f64(old) + gf
    return y

@@ -1,0 +1,179 @@
+from contextlib import ExitStack
+
+import concourse.mybir as mybir
+
+F32 = mybir.dt.float32
+BF16 = mybir.dt.bfloat16
+I32 = mybir.dt.int32
+U32 = mybir.dt.uint32
+U16 = mybir.dt.uint16
+U8 = mybir.dt.uint8
+FP8X4 = mybir.dt.float8_e4m3fn_x4
+ALU = mybir.AluOpType
+ACT = mybir.ActivationFunctionType
+
+P = 128
+PACK = 4
+FEATURES = 512
+TOKENS = 2048
+SLOTS = 512
+ROWS = 128
+HALF = SLOTS // 2
+OUT_CHUNK = 512
+KEY_SCALE_ROW = 0
+VAL_SCALE_ROW = 4
+
+FLOPS = 2 * 2 * FEATURES * ROWS * SLOTS
+
+
+def load_scales(queue, plane, scales, first_row):
+    for quad in range(4):
+        row = 32 * quad + first_row
+        queue.dma_start(out=plane[row : row + 4, :].bitcast(I32), in_=scales[0, 4 * quad : 4 * quad + 4, :].bitcast(I32))
+
+
+def load_words(nc, window, words):
+    nc.sync.dma_start(out=window[:].bitcast(I32), in_=words[0].rearrange("p n t -> p (n t)").bitcast(I32))
+
+
+def interleave(nc, grouped, raw):
+    nc.scalar.copy(
+        out=grouped[:].rearrange("p (c i) t -> p c t i", i=4),
+        in_=raw[:].rearrange("p t (c i) -> p c t i", i=4),
+    )
+
+
+def quantize(nc, codes, plane, grouped):
+    nc.vector.quantize_mx(out=codes[:].bitcast(FP8X4), scales=plane[:], in_=grouped[:].rearrange("p w t -> p (w t)"))
+
+
+def tile_attend_bsquareshares_s_kernel(
+    tc, query, keys_words, keys_scales, floor, reserve, gout, vals_words, vals_scales, old, offs, out
+):
+    nc = tc.nc
+    with ExitStack() as ctx:
+        sb = ctx.enter_context(tc.tile_pool(name="sb", bufs=1))
+        psum = ctx.enter_context(tc.psum_pool(name="psum", bufs=1))
+
+        offsets = sb.tile([P, SLOTS // 16], U16, name="offsets")
+        key_words = sb.tile([P, TOKENS], U32, name="key_words")
+        val_words = sb.tile([P, TOKENS], U32, name="val_words")
+        key_plane = sb.tile([P, TOKENS], U8, name="key_plane")
+        val_plane = sb.tile([P, TOKENS], U8, name="val_plane")
+        placed = sb.tile([P, TOKENS], F32, name="placed")
+        query_raw = sb.tile([P, PACK, ROWS], F32, name="query_raw", tag="query_then_old")
+        gout_raw = sb.tile([P, PACK, ROWS], F32, name="gout_raw")
+        floor_col = sb.tile([P, 1], F32, name="floor_col")
+        reserve_col = sb.tile([P, 1], F32, name="reserve_col")
+
+        nc.vector.memset(key_plane[:].bitcast(I32), 0)
+        nc.vector.memset(val_plane[:].bitcast(I32), 0)
+        nc.vector.memset(placed[:], 0.0)
+
+        nc.sync.dma_start(offsets[:], offs)
+        nc.sync.dma_start(out=query_raw[:], in_=query.rearrange("(p t) w -> p t w", t=PACK))
+        load_scales(nc.sync, key_plane, keys_scales, KEY_SCALE_ROW)
+        load_words(nc, key_words, keys_words)
+        nc.sync.dma_start(out=gout_raw[:], in_=gout.rearrange("(p t) w -> p t w", t=PACK))
+        load_scales(nc.sync, val_plane, vals_scales, VAL_SCALE_ROW)
+        load_words(nc, val_words, vals_words)
+        nc.gpsimd.dma_start(out=floor_col[:], in_=floor)
+        nc.gpsimd.dma_start(out=reserve_col[:], in_=reserve)
+
+        key_scales_g = sb.tile([P, SLOTS], U8, name="key_scales_g", align_bytes=64)
+        key_words_g = sb.tile([P, SLOTS], U32, name="key_words_g", align_bytes=64)
+        nc.vector.tensor_copy(key_scales_g[:], key_plane[:].indirect(offsets[:]))
+
+        query_bf = sb.tile([P, ROWS, PACK], BF16, name="query_bf", align_bytes=64)
+        query_codes = sb.tile([P, ROWS], U32, name="query_codes", align_bytes=64)
+        query_plane = sb.tile([P, ROWS], U8, name="query_plane", align_bytes=64)
+        interleave(nc, query_bf, query_raw)
+        quantize(nc, query_codes, query_plane, query_bf)
+        nc.vector.tensor_copy(key_words_g[:], key_words[:].indirect(offsets[:]))
+
+        old_sb = sb.tile([P, TOKENS], F32, name="old_sb", tag="query_then_old")
+        nc.sync.dma_start(out=old_sb[:], in_=old)
+
+        a_ps = psum.tile([P, SLOTS], F32, name="a_ps")
+        nc.tensor.matmul_mx(
+            out=a_ps[:],
+            lhsT=query_codes[:].bitcast(FP8X4),
+            lhsT_scale=query_plane[:],
+            rhs=key_words_g[:].bitcast(FP8X4),
+            rhs_scale=key_scales_g[KEY_SCALE_ROW:P, :],
+            start=True,
+            stop=True,
+        )
+
+        gout_bf = sb.tile([P, ROWS, PACK], BF16, name="gout_bf", align_bytes=64)
+        gout_codes = sb.tile([P, ROWS], U32, name="gout_codes", align_bytes=64)
+        gout_plane = sb.tile([P, ROWS], U8, name="gout_plane", align_bytes=64)
+        interleave(nc, gout_bf, gout_raw)
+        val_scales_g = sb.tile([P, SLOTS], U8, name="val_scales_g", align_bytes=64)
+        nc.vector.tensor_copy(val_scales_g[:], val_plane[:].indirect(offsets[:]))
+        quantize(nc, gout_codes, gout_plane, gout_bf)
+
+        neg_reserve = sb.tile([P, 1], F32, name="neg_reserve")
+        neg_base = sb.tile([P, 1], F32, name="neg_base")
+        nc.scalar.activation(neg_reserve[:], reserve_col[:], ACT.Copy, scale=-1.0)
+        nc.scalar.activation(neg_base[:], floor_col[:], ACT.Identity, scale=-float(SLOTS), bias=neg_reserve[:])
+
+        a_sq = sb.tile([P, SLOTS], F32, name="a_sq")
+        sum_sq = sb.tile([P, 1], F32, name="sum_sq")
+        neg_z = sb.tile([P, 1], F32, name="neg_z")
+        neg_inv_z = sb.tile([P, 1], F32, name="neg_inv_z")
+        inv_z_1024 = sb.tile([P, 1], F32, name="inv_z_1024")
+        a_factor = sb.tile([P, 1], F32, name="a_factor")
+        a_scaled = sb.tile([P, SLOTS], F32, name="a_scaled")
+        nc.scalar.activation(a_sq[:], a_ps[:], ACT.Square, accum_out=sum_sq[:])
+        nc.scalar.activation(neg_z[:], sum_sq[:], ACT.Identity, scale=-1.0, bias=neg_base[:])
+        nc.vector.reciprocal(neg_inv_z[:], neg_z[:])
+        nc.scalar.activation(inv_z_1024[:], neg_inv_z[:], ACT.Copy, scale=-1024.0)
+        nc.scalar.activation(a_factor[:], neg_inv_z[:], ACT.Copy, scale=inv_z_1024[:])
+        nc.scalar.activation(a_scaled[:], a_ps[:], ACT.Copy, scale=a_factor[:])
+
+        c_ps = []
+        for h in range(2):
+            val_words_g = sb.tile([P, HALF], U32, name="val_words_g%d" % h, align_bytes=64)
+            nc.vector.tensor_copy(val_words_g[:], val_words[:].indirect(offsets[:, 16 * h : 16 * (h + 1)]))
+            bank = psum.tile([P, HALF], F32, name="c_ps%d" % h)
+            nc.tensor.matmul_mx(
+                out=bank[:],
+                lhsT=gout_codes[:].bitcast(FP8X4),
+                lhsT_scale=gout_plane[:],
+                rhs=val_words_g[:].bitcast(FP8X4),
+                rhs_scale=val_scales_g[VAL_SCALE_ROW:P, HALF * h : HALF * (h + 1)],
+                start=True,
+                stop=True,
+            )
+            c_ps.append(bank)
+
+        cz_first = sb.tile([P, HALF], F32, name="cz_first")
+        nc.scalar.activation(cz_first[:], c_ps[0][:], ACT.Copy, scale=neg_z[:])
+
+        sums = []
+        for h in range(2):
+            cp = sb.tile([P, HALF], F32, name="cp%d" % h)
+            cp_sum = sb.tile([P, 1], F32, name="cp_sum%d" % h)
+            nc.vector.scalar_tensor_tensor(
+                cp[:], a_sq[:, HALF * h : HALF * (h + 1)], floor_col[:], c_ps[h][:], ALU.add, ALU.mult, accum_out=cp_sum[:]
+            )
+            sums.append(cp_sum)
+
+        t_first = sb.tile([P, HALF], F32, name="t_first")
+        nc.vector.tensor_scalar(t_first[:], cz_first[:], sums[0][:], sums[1][:], ALU.add, ALU.add)
+        cp_total = sb.tile([P, 1], F32, name="cp_total")
+        t_second = sb.tile([P, HALF], F32, name="t_second")
+        nc.scalar.activation(cp_total[:], sums[0][:], ACT.Identity, bias=sums[1][:])
+        nc.scalar.activation(t_second[:], c_ps[1][:], ACT.Identity, scale=neg_z[:], bias=cp_total[:])
+
+        for h, t_half in enumerate((t_first, t_second)):
+            nc.vector.tensor_tensor(
+                placed[:].indirect(offsets[:, 16 * h : 16 * (h + 1)]), a_scaled[:, HALF * h : HALF * (h + 1)], t_half[:], ALU.mult
+            )
+
+        for c in range(TOKENS // OUT_CHUNK):
+            cols = slice(c * OUT_CHUNK, (c + 1) * OUT_CHUNK)
+            result = sb.tile([P, OUT_CHUNK], F32, name="result%d" % c)
+            nc.vector.tensor_tensor(result[:], placed[:, cols], old_sb[:, cols], ALU.add)
+            nc.sync.dma_start(out=out[:, cols], in_=result[:])

@@ -19,7 +19,7 @@ TOKENS = 2048
 SLOTS = 512
 ROWS = 128
 HALF = SLOTS // 2
-OUT_CHUNK = 512
+OUT_WIDTHS = (576, 512, 448, 320, 192)
 KEY_SCALE_ROW = 0
 VAL_SCALE_ROW = 4
 
@@ -57,7 +57,7 @@ def tile_attend_bsquareshares_s_kernel(
 
         offsets = sb.tile([P, SLOTS // 16], U16, name="offsets")
         key_words = sb.tile([P, TOKENS], U32, name="key_words")
-        val_words = sb.tile([P, TOKENS], U32, name="val_words")
+        val_words = sb.tile([P, TOKENS], U32, name="val_words", tag="values_then_inv_z")
         key_plane = sb.tile([P, TOKENS], U8, name="key_plane")
         val_plane = sb.tile([P, TOKENS], U8, name="val_plane")
         placed = sb.tile([P, TOKENS], F32, name="placed")
@@ -66,19 +66,20 @@ def tile_attend_bsquareshares_s_kernel(
         floor_col = sb.tile([P, 1], F32, name="floor_col")
         reserve_col = sb.tile([P, 1], F32, name="reserve_col")
 
-        nc.vector.memset(key_plane[:].bitcast(I32), 0)
+        nc.gpsimd.memset(key_plane[:, : TOKENS // 2].bitcast(I32), 0)
+        nc.vector.memset(key_plane[:, TOKENS // 2 :].bitcast(I32), 0)
         nc.vector.memset(val_plane[:].bitcast(I32), 0)
         nc.vector.memset(placed[:], 0.0)
 
         nc.sync.dma_start(offsets[:], offs)
         nc.sync.dma_start(out=query_raw[:], in_=query.rearrange("(p t) w -> p t w", t=PACK))
+        nc.sync.dma_start(out=gout_raw[:], in_=gout.rearrange("(p t) w -> p t w", t=PACK))
         load_scales(nc.sync, key_plane, keys_scales, KEY_SCALE_ROW)
         load_words(nc, key_words, keys_words)
-        nc.sync.dma_start(out=gout_raw[:], in_=gout.rearrange("(p t) w -> p t w", t=PACK))
+        nc.sync.dma_start(out=floor_col[:], in_=floor)
+        nc.sync.dma_start(out=reserve_col[:], in_=reserve)
         load_scales(nc.sync, val_plane, vals_scales, VAL_SCALE_ROW)
         load_words(nc, val_words, vals_words)
-        nc.gpsimd.dma_start(out=floor_col[:], in_=floor)
-        nc.gpsimd.dma_start(out=reserve_col[:], in_=reserve)
 
         key_scales_g = sb.tile([P, SLOTS], U8, name="key_scales_g", align_bytes=64)
         key_words_g = sb.tile([P, SLOTS], U32, name="key_words_g", align_bytes=64)
@@ -88,7 +89,12 @@ def tile_attend_bsquareshares_s_kernel(
         query_codes = sb.tile([P, ROWS], U32, name="query_codes", align_bytes=64)
         query_plane = sb.tile([P, ROWS], U8, name="query_plane", align_bytes=64)
         interleave(nc, query_bf, query_raw)
+        gout_bf = sb.tile([P, ROWS, PACK], BF16, name="gout_bf", align_bytes=64)
+        gout_codes = sb.tile([P, ROWS], U32, name="gout_codes", align_bytes=64)
+        gout_plane = sb.tile([P, ROWS], U8, name="gout_plane", align_bytes=64)
+        interleave(nc, gout_bf, gout_raw)
         quantize(nc, query_codes, query_plane, query_bf)
+        quantize(nc, gout_codes, gout_plane, gout_bf)
         nc.vector.tensor_copy(key_words_g[:], key_words[:].indirect(offsets[:]))
 
         old_sb = sb.tile([P, TOKENS], F32, name="old_sb", tag="query_then_old")
@@ -105,32 +111,16 @@ def tile_attend_bsquareshares_s_kernel(
             stop=True,
         )
 
-        gout_bf = sb.tile([P, ROWS, PACK], BF16, name="gout_bf", align_bytes=64)
-        gout_codes = sb.tile([P, ROWS], U32, name="gout_codes", align_bytes=64)
-        gout_plane = sb.tile([P, ROWS], U8, name="gout_plane", align_bytes=64)
-        interleave(nc, gout_bf, gout_raw)
         val_scales_g = sb.tile([P, SLOTS], U8, name="val_scales_g", align_bytes=64)
         nc.vector.tensor_copy(val_scales_g[:], val_plane[:].indirect(offsets[:]))
-        quantize(nc, gout_codes, gout_plane, gout_bf)
-
-        neg_reserve = sb.tile([P, 1], F32, name="neg_reserve")
-        neg_base = sb.tile([P, 1], F32, name="neg_base")
-        nc.scalar.activation(neg_reserve[:], reserve_col[:], ACT.Copy, scale=-1.0)
-        nc.scalar.activation(neg_base[:], floor_col[:], ACT.Identity, scale=-float(SLOTS), bias=neg_reserve[:])
 
         a_sq = sb.tile([P, SLOTS], F32, name="a_sq")
         sum_sq = sb.tile([P, 1], F32, name="sum_sq")
-        neg_z = sb.tile([P, 1], F32, name="neg_z")
-        neg_inv_z = sb.tile([P, 1], F32, name="neg_inv_z")
-        inv_z_1024 = sb.tile([P, 1], F32, name="inv_z_1024")
-        a_factor = sb.tile([P, 1], F32, name="a_factor")
-        a_scaled = sb.tile([P, SLOTS], F32, name="a_scaled")
+        base = sb.tile([P, 1], F32, name="base")
+        z = sb.tile([P, 1], F32, name="z")
         nc.scalar.activation(a_sq[:], a_ps[:], ACT.Square, accum_out=sum_sq[:])
-        nc.scalar.activation(neg_z[:], sum_sq[:], ACT.Identity, scale=-1.0, bias=neg_base[:])
-        nc.vector.reciprocal(neg_inv_z[:], neg_z[:])
-        nc.scalar.activation(inv_z_1024[:], neg_inv_z[:], ACT.Copy, scale=-1024.0)
-        nc.scalar.activation(a_factor[:], neg_inv_z[:], ACT.Copy, scale=inv_z_1024[:])
-        nc.scalar.activation(a_scaled[:], a_ps[:], ACT.Copy, scale=a_factor[:])
+        nc.scalar.activation(base[:], floor_col[:], ACT.Identity, scale=float(SLOTS), bias=reserve_col[:])
+        nc.scalar.activation(z[:], sum_sq[:], ACT.Identity, bias=base[:])
 
         c_ps = []
         for h in range(2):
@@ -148,32 +138,50 @@ def tile_attend_bsquareshares_s_kernel(
             )
             c_ps.append(bank)
 
-        cz_first = sb.tile([P, HALF], F32, name="cz_first")
-        nc.scalar.activation(cz_first[:], c_ps[0][:], ACT.Copy, scale=neg_z[:])
+        inv_z = sb.tile([P, 1], F32, name="inv_z", tag="values_then_inv_z")
+        a_factor = sb.tile([P, 1], F32, name="a_factor")
+        nc.vector.reciprocal(inv_z[:], z[:])
+        nc.scalar.activation(a_factor[:], inv_z[:], ACT.Square, scale=32.0)
 
-        sums = []
-        for h in range(2):
+        def scaled_a(h):
+            tile = sb.tile([P, HALF], F32, name="a_scaled%d" % h)
+            nc.scalar.activation(tile[:], a_ps[:, HALF * h : HALF * (h + 1)], ACT.Copy, scale=a_factor[:])
+            return tile
+
+        def weighted_sum(h):
             cp = sb.tile([P, HALF], F32, name="cp%d" % h)
             cp_sum = sb.tile([P, 1], F32, name="cp_sum%d" % h)
             nc.vector.scalar_tensor_tensor(
                 cp[:], a_sq[:, HALF * h : HALF * (h + 1)], floor_col[:], c_ps[h][:], ALU.add, ALU.mult, accum_out=cp_sum[:]
             )
-            sums.append(cp_sum)
+            return cp_sum
+
+        def scatter(h, a_half, t_half):
+            nc.vector.tensor_tensor(placed[:].indirect(offsets[:, 16 * h : 16 * (h + 1)]), a_half[:], t_half[:], ALU.mult)
+
+        a_first = scaled_a(0)
+        sum_first = weighted_sum(0)
+        cz_first = sb.tile([P, HALF], F32, name="cz_first")
+        nc.scalar.activation(cz_first[:], c_ps[0][:], ACT.Copy, scale=z[:])
+        sum_second = weighted_sum(1)
 
         t_first = sb.tile([P, HALF], F32, name="t_first")
-        nc.vector.tensor_scalar(t_first[:], cz_first[:], sums[0][:], sums[1][:], ALU.add, ALU.add)
+        nc.vector.tensor_scalar(t_first[:], cz_first[:], sum_first[:], sum_second[:], ALU.subtract, ALU.subtract)
+        scatter(0, a_first, t_first)
+
+        a_second = scaled_a(1)
         cp_total = sb.tile([P, 1], F32, name="cp_total")
+        neg_cp_total = sb.tile([P, 1], F32, name="neg_cp_total")
         t_second = sb.tile([P, HALF], F32, name="t_second")
-        nc.scalar.activation(cp_total[:], sums[0][:], ACT.Identity, bias=sums[1][:])
-        nc.scalar.activation(t_second[:], c_ps[1][:], ACT.Identity, scale=neg_z[:], bias=cp_total[:])
+        nc.scalar.activation(cp_total[:], sum_first[:], ACT.Identity, bias=sum_second[:])
+        nc.scalar.activation(neg_cp_total[:], cp_total[:], ACT.Copy, scale=-1.0)
+        nc.scalar.activation(t_second[:], c_ps[1][:], ACT.Identity, scale=z[:], bias=neg_cp_total[:])
+        scatter(1, a_second, t_second)
 
-        for h, t_half in enumerate((t_first, t_second)):
-            nc.vector.tensor_tensor(
-                placed[:].indirect(offsets[:, 16 * h : 16 * (h + 1)]), a_scaled[:, HALF * h : HALF * (h + 1)], t_half[:], ALU.mult
-            )
-
-        for c in range(TOKENS // OUT_CHUNK):
-            cols = slice(c * OUT_CHUNK, (c + 1) * OUT_CHUNK)
-            result = sb.tile([P, OUT_CHUNK], F32, name="result%d" % c)
+        first = 0
+        for c, width in enumerate(OUT_WIDTHS):
+            cols = slice(first, first + width)
+            first = first + width
+            result = sb.tile([P, width], F32, name="result%d" % c)
             nc.vector.tensor_tensor(result[:], placed[:, cols], old_sb[:, cols], ALU.add)
             nc.sync.dma_start(out=out[:, cols], in_=result[:])

@@ -27,9 +27,8 @@ FLOPS = 2 * 2 * FEATURES * ROWS * SLOTS
 
 
 def load_scales(queue, plane, scales, first_row):
-    for quad in range(4):
-        row = 32 * quad + first_row
-        queue.dma_start(out=plane[row : row + 4, :].bitcast(I32), in_=scales[0, 4 * quad : 4 * quad + 4, :].bitcast(I32))
+    for row in range(4):
+        queue.dma_start(out=plane[first_row + row : P : 32, :].bitcast(I32), in_=scales[0, row:16:4, :].bitcast(I32))
 
 
 def load_words(nc, window, words):
@@ -62,7 +61,7 @@ def tile_attend_bsquareshares_s_kernel(
         val_plane = sb.tile([P, TOKENS], U8, name="val_plane")
         placed = sb.tile([P, TOKENS], F32, name="placed")
         query_raw = sb.tile([P, PACK, ROWS], F32, name="query_raw", tag="query_then_old")
-        gout_raw = sb.tile([P, PACK, ROWS], F32, name="gout_raw")
+        gout_raw = sb.tile([P, PACK, ROWS], F32, name="gout_raw", tag="gout_then_a_sq")
         floor_col = sb.tile([P, 1], F32, name="floor_col")
         reserve_col = sb.tile([P, 1], F32, name="reserve_col")
 
@@ -73,11 +72,11 @@ def tile_attend_bsquareshares_s_kernel(
 
         nc.sync.dma_start(offsets[:], offs)
         nc.sync.dma_start(out=query_raw[:], in_=query.rearrange("(p t) w -> p t w", t=PACK))
-        nc.sync.dma_start(out=gout_raw[:], in_=gout.rearrange("(p t) w -> p t w", t=PACK))
+        nc.sync.dma_start(out=floor_col[:], in_=floor)
         load_scales(nc.sync, key_plane, keys_scales, KEY_SCALE_ROW)
         load_words(nc, key_words, keys_words)
-        nc.sync.dma_start(out=floor_col[:], in_=floor)
         nc.sync.dma_start(out=reserve_col[:], in_=reserve)
+        nc.sync.dma_start(out=gout_raw[:], in_=gout.rearrange("(p t) w -> p t w", t=PACK))
         load_scales(nc.sync, val_plane, vals_scales, VAL_SCALE_ROW)
         load_words(nc, val_words, vals_words)
 
@@ -94,7 +93,6 @@ def tile_attend_bsquareshares_s_kernel(
         gout_plane = sb.tile([P, ROWS], U8, name="gout_plane", align_bytes=64)
         interleave(nc, gout_bf, gout_raw)
         quantize(nc, query_codes, query_plane, query_bf)
-        quantize(nc, gout_codes, gout_plane, gout_bf)
         nc.vector.tensor_copy(key_words_g[:], key_words[:].indirect(offsets[:]))
 
         old_sb = sb.tile([P, TOKENS], F32, name="old_sb", tag="query_then_old")
@@ -113,8 +111,9 @@ def tile_attend_bsquareshares_s_kernel(
 
         val_scales_g = sb.tile([P, SLOTS], U8, name="val_scales_g", align_bytes=64)
         nc.vector.tensor_copy(val_scales_g[:], val_plane[:].indirect(offsets[:]))
+        quantize(nc, gout_codes, gout_plane, gout_bf)
 
-        a_sq = sb.tile([P, SLOTS], F32, name="a_sq")
+        a_sq = sb.tile([P, SLOTS], F32, name="a_sq", tag="gout_then_a_sq")
         sum_sq = sb.tile([P, 1], F32, name="sum_sq")
         base = sb.tile([P, 1], F32, name="base")
         z = sb.tile([P, 1], F32, name="z")
@@ -144,12 +143,12 @@ def tile_attend_bsquareshares_s_kernel(
         nc.scalar.activation(a_factor[:], inv_z[:], ACT.Square, scale=32.0)
 
         def scaled_a(h):
-            tile = sb.tile([P, HALF], F32, name="a_scaled%d" % h)
+            tile = sb.tile([P, HALF], F32, name="a_scaled%d" % h, tag="cp_then_a_scaled%d" % h)
             nc.scalar.activation(tile[:], a_ps[:, HALF * h : HALF * (h + 1)], ACT.Copy, scale=a_factor[:])
             return tile
 
         def weighted_sum(h):
-            cp = sb.tile([P, HALF], F32, name="cp%d" % h)
+            cp = sb.tile([P, HALF], F32, name="cp%d" % h, tag="cp_then_a_scaled%d" % h)
             cp_sum = sb.tile([P, 1], F32, name="cp_sum%d" % h)
             nc.vector.scalar_tensor_tensor(
                 cp[:], a_sq[:, HALF * h : HALF * (h + 1)], floor_col[:], c_ps[h][:], ALU.add, ALU.mult, accum_out=cp_sum[:]
@@ -159,10 +158,10 @@ def tile_attend_bsquareshares_s_kernel(
         def scatter(h, a_half, t_half):
             nc.vector.tensor_tensor(placed[:].indirect(offsets[:, 16 * h : 16 * (h + 1)]), a_half[:], t_half[:], ALU.mult)
 
-        a_first = scaled_a(0)
         sum_first = weighted_sum(0)
         cz_first = sb.tile([P, HALF], F32, name="cz_first")
         nc.scalar.activation(cz_first[:], c_ps[0][:], ACT.Copy, scale=z[:])
+        a_first = scaled_a(0)
         sum_second = weighted_sum(1)
 
         t_first = sb.tile([P, HALF], F32, name="t_first")

@@ -20,15 +20,18 @@ SLOTS = 512
 ROWS = 128
 HALF = SLOTS // 2
 OUT_WIDTHS = (576, 512, 448, 320, 192)
-KEY_SCALE_ROW = 0
-VAL_SCALE_ROW = 4
 
 FLOPS = 2 * 2 * FEATURES * ROWS * SLOTS
 
 
-def load_scales(queue, plane, scales, first_row):
-    for row in range(4):
-        queue.dma_start(out=plane[first_row + row : P : 32, :].bitcast(I32), in_=scales[0, row:16:4, :].bitcast(I32))
+def load_scales(nc, window, scales):
+    nc.sync.dma_start(out=window[0:P:8, :].bitcast(I32), in_=scales[0].bitcast(I32))
+
+
+def place_scales(nc, plane, gathered):
+    nc.vector.tensor_copy(plane[:].bitcast(I32), gathered[:].bitcast(I32))
+    for row in range(1, 4):
+        nc.scalar.dma_start(out=plane[row:P:32, :].bitcast(I32), in_=gathered[8 * row : P : 32, :].bitcast(I32))
 
 
 def load_words(nc, window, words):
@@ -55,13 +58,13 @@ def tile_attend_bsquareshares_s_kernel(
         psum = ctx.enter_context(tc.psum_pool(name="psum", bufs=1))
 
         offsets = sb.tile([P, SLOTS // 16], U16, name="offsets")
-        key_words = sb.tile([P, TOKENS], U32, name="key_words")
+        key_words = sb.tile([P, TOKENS], U32, name="key_words", tag="keys_then_old")
         val_words = sb.tile([P, TOKENS], U32, name="val_words", tag="values_then_inv_z")
         key_plane = sb.tile([P, TOKENS], U8, name="key_plane")
         val_plane = sb.tile([P, TOKENS], U8, name="val_plane")
         placed = sb.tile([P, TOKENS], F32, name="placed")
-        query_raw = sb.tile([P, PACK, ROWS], F32, name="query_raw", tag="query_then_old")
-        gout_raw = sb.tile([P, PACK, ROWS], F32, name="gout_raw", tag="gout_then_a_sq")
+        query_raw = sb.tile([P, PACK, ROWS], F32, name="query_raw", tag="query_then_plane", align_bytes=64)
+        gout_raw = sb.tile([P, PACK, ROWS], F32, name="gout_raw", tag="gout_then_plane", align_bytes=64)
         floor_col = sb.tile([P, 1], F32, name="floor_col")
         reserve_col = sb.tile([P, 1], F32, name="reserve_col")
 
@@ -71,31 +74,39 @@ def tile_attend_bsquareshares_s_kernel(
         nc.vector.memset(placed[:], 0.0)
 
         nc.sync.dma_start(offsets[:], offs)
-        nc.sync.dma_start(out=query_raw[:], in_=query.rearrange("(p t) w -> p t w", t=PACK))
         nc.sync.dma_start(out=floor_col[:], in_=floor)
-        load_scales(nc.sync, key_plane, keys_scales, KEY_SCALE_ROW)
-        load_words(nc, key_words, keys_words)
         nc.sync.dma_start(out=reserve_col[:], in_=reserve)
+        nc.sync.dma_start(out=query_raw[:], in_=query.rearrange("(p t) w -> p t w", t=PACK))
+        load_scales(nc, key_plane, keys_scales)
         nc.sync.dma_start(out=gout_raw[:], in_=gout.rearrange("(p t) w -> p t w", t=PACK))
-        load_scales(nc.sync, val_plane, vals_scales, VAL_SCALE_ROW)
+        load_scales(nc, val_plane, vals_scales)
+        load_words(nc, key_words, keys_words)
         load_words(nc, val_words, vals_words)
-
-        key_scales_g = sb.tile([P, SLOTS], U8, name="key_scales_g", align_bytes=64)
-        key_words_g = sb.tile([P, SLOTS], U32, name="key_words_g", align_bytes=64)
-        nc.vector.tensor_copy(key_scales_g[:], key_plane[:].indirect(offsets[:]))
 
         query_bf = sb.tile([P, ROWS, PACK], BF16, name="query_bf", align_bytes=64)
         query_codes = sb.tile([P, ROWS], U32, name="query_codes", align_bytes=64)
         query_plane = sb.tile([P, ROWS], U8, name="query_plane", align_bytes=64)
-        interleave(nc, query_bf, query_raw)
         gout_bf = sb.tile([P, ROWS, PACK], BF16, name="gout_bf", align_bytes=64)
         gout_codes = sb.tile([P, ROWS], U32, name="gout_codes", align_bytes=64)
         gout_plane = sb.tile([P, ROWS], U8, name="gout_plane", align_bytes=64)
+        interleave(nc, query_bf, query_raw)
         interleave(nc, gout_bf, gout_raw)
+
+        key_rows_g = sb.tile([P, SLOTS], U8, name="key_rows_g")
+        key_scales_g = sb.tile([P, SLOTS], U8, name="key_scales_g", tag="query_then_plane", align_bytes=64)
+        nc.vector.tensor_copy(key_rows_g[:], key_plane[:].indirect(offsets[:]))
+        place_scales(nc, key_scales_g, key_rows_g)
+        val_rows_g = sb.tile([P, SLOTS], U8, name="val_rows_g")
+        val_scales_g = sb.tile([P, SLOTS], U8, name="val_scales_g", tag="gout_then_plane", align_bytes=64)
+        nc.vector.tensor_copy(val_rows_g[:], val_plane[:].indirect(offsets[:]))
+        place_scales(nc, val_scales_g, val_rows_g)
+
         quantize(nc, query_codes, query_plane, query_bf)
+        quantize(nc, gout_codes, gout_plane, gout_bf)
+        key_words_g = sb.tile([P, SLOTS], U32, name="key_words_g", align_bytes=64)
         nc.vector.tensor_copy(key_words_g[:], key_words[:].indirect(offsets[:]))
 
-        old_sb = sb.tile([P, TOKENS], F32, name="old_sb", tag="query_then_old")
+        old_sb = sb.tile([P, TOKENS], F32, name="old_sb", tag="keys_then_old")
         nc.sync.dma_start(out=old_sb[:], in_=old)
 
         a_ps = psum.tile([P, SLOTS], F32, name="a_ps")
@@ -104,21 +115,17 @@ def tile_attend_bsquareshares_s_kernel(
             lhsT=query_codes[:].bitcast(FP8X4),
             lhsT_scale=query_plane[:],
             rhs=key_words_g[:].bitcast(FP8X4),
-            rhs_scale=key_scales_g[KEY_SCALE_ROW:P, :],
+            rhs_scale=key_scales_g[:],
             start=True,
             stop=True,
         )
 
-        val_scales_g = sb.tile([P, SLOTS], U8, name="val_scales_g", align_bytes=64)
-        nc.vector.tensor_copy(val_scales_g[:], val_plane[:].indirect(offsets[:]))
-        quantize(nc, gout_codes, gout_plane, gout_bf)
-
-        a_sq = sb.tile([P, SLOTS], F32, name="a_sq", tag="gout_then_a_sq")
+        a_sq = sb.tile([P, SLOTS], F32, name="a_sq")
         sum_sq = sb.tile([P, 1], F32, name="sum_sq")
         base = sb.tile([P, 1], F32, name="base")
         z = sb.tile([P, 1], F32, name="z")
         nc.scalar.activation(a_sq[:], a_ps[:], ACT.Square, accum_out=sum_sq[:])
-        nc.scalar.activation(base[:], floor_col[:], ACT.Identity, scale=float(SLOTS), bias=reserve_col[:])
+        nc.gpsimd.tensor_scalar(base[:], floor_col[:], float(SLOTS), reserve_col[:], ALU.mult, ALU.add)
         nc.scalar.activation(z[:], sum_sq[:], ACT.Identity, bias=base[:])
 
         c_ps = []
@@ -131,7 +138,7 @@ def tile_attend_bsquareshares_s_kernel(
                 lhsT=gout_codes[:].bitcast(FP8X4),
                 lhsT_scale=gout_plane[:],
                 rhs=val_words_g[:].bitcast(FP8X4),
-                rhs_scale=val_scales_g[VAL_SCALE_ROW:P, HALF * h : HALF * (h + 1)],
+                rhs_scale=val_scales_g[:, HALF * h : HALF * (h + 1)],
                 start=True,
                 stop=True,
             )

@@ -59,7 +59,7 @@ def tile_attend_bsquareshares_s_kernel(
 
         offsets = sb.tile([P, SLOTS // 16], U16, name="offsets")
         key_words = sb.tile([P, TOKENS], U32, name="key_words", tag="keys_then_old")
-        val_words = sb.tile([P, TOKENS], U32, name="val_words", tag="values_then_inv_z")
+        val_words = sb.tile([P, TOKENS], U32, name="val_words")
         key_plane = sb.tile([P, TOKENS], U8, name="key_plane")
         val_plane = sb.tile([P, TOKENS], U8, name="val_plane")
         placed = sb.tile([P, TOKENS], F32, name="placed")
@@ -144,50 +144,47 @@ def tile_attend_bsquareshares_s_kernel(
             )
             c_ps.append(bank)
 
-        inv_z = sb.tile([P, 1], F32, name="inv_z", tag="values_then_inv_z")
-        a_factor = sb.tile([P, 1], F32, name="a_factor")
-        nc.vector.reciprocal(inv_z[:], z[:])
-        nc.scalar.activation(a_factor[:], inv_z[:], ACT.Square, scale=32.0)
-
-        def scaled_a(h):
-            tile = sb.tile([P, HALF], F32, name="a_scaled%d" % h, tag="cp_then_a_scaled%d" % h)
-            nc.scalar.activation(tile[:], a_ps[:, HALF * h : HALF * (h + 1)], ACT.Copy, scale=a_factor[:])
-            return tile
+        a_sb = sb.tile([P, SLOTS], F32, name="a_sb")
+        nc.scalar.copy(a_sb[:], a_ps[:])
 
         def weighted_sum(h):
-            cp = sb.tile([P, HALF], F32, name="cp%d" % h, tag="cp_then_a_scaled%d" % h)
+            cp = sb.tile([P, HALF], F32, name="cp%d" % h)
             cp_sum = sb.tile([P, 1], F32, name="cp_sum%d" % h)
             nc.vector.scalar_tensor_tensor(
                 cp[:], a_sq[:, HALF * h : HALF * (h + 1)], floor_col[:], c_ps[h][:], ALU.add, ALU.mult, accum_out=cp_sum[:]
             )
             return cp_sum
 
-        def scatter(h, a_half, t_half):
-            nc.vector.tensor_tensor(placed[:].indirect(offsets[:, 16 * h : 16 * (h + 1)]), a_half[:], t_half[:], ALU.mult)
+        def scatter(h, t_half):
+            nc.vector.tensor_tensor(
+                placed[:].indirect(offsets[:, 16 * h : 16 * (h + 1)]), a_sb[:, HALF * h : HALF * (h + 1)], t_half[:], ALU.mult
+            )
 
         sum_first = weighted_sum(0)
         cz_first = sb.tile([P, HALF], F32, name="cz_first")
         nc.scalar.activation(cz_first[:], c_ps[0][:], ACT.Copy, scale=z[:])
-        a_first = scaled_a(0)
         sum_second = weighted_sum(1)
 
-        t_first = sb.tile([P, HALF], F32, name="t_first")
+        t_first = sb.tile([P, HALF], F32, name="t_first", tag="t_first_then_inv_z")
         nc.vector.tensor_scalar(t_first[:], cz_first[:], sum_first[:], sum_second[:], ALU.subtract, ALU.subtract)
-        scatter(0, a_first, t_first)
+        scatter(0, t_first)
 
-        a_second = scaled_a(1)
         cp_total = sb.tile([P, 1], F32, name="cp_total")
         neg_cp_total = sb.tile([P, 1], F32, name="neg_cp_total")
         t_second = sb.tile([P, HALF], F32, name="t_second")
         nc.scalar.activation(cp_total[:], sum_first[:], ACT.Identity, bias=sum_second[:])
         nc.scalar.activation(neg_cp_total[:], cp_total[:], ACT.Copy, scale=-1.0)
         nc.scalar.activation(t_second[:], c_ps[1][:], ACT.Identity, scale=z[:], bias=neg_cp_total[:])
-        scatter(1, a_second, t_second)
+        inv_z = sb.tile([P, 1], F32, name="inv_z", tag="t_first_then_inv_z")
+        row_factor = sb.tile([P, 1], F32, name="row_factor")
+        nc.vector.reciprocal(inv_z[:], z[:])
+        nc.scalar.activation(row_factor[:], inv_z[:], ACT.Square, scale=32.0)
+        scatter(1, t_second)
 
         first = 0
         for c, width in enumerate(OUT_WIDTHS):
             cols = slice(first, first + width)
             first = first + width
             result = sb.tile([P, width], F32, name="result%d" % c)
-            nc.vector.tensor_tensor(result[:], placed[:, cols], old_sb[:, cols], ALU.add)
+            nc.vector.scalar_tensor_tensor(result[:], placed[:, cols], row_factor[:], old_sb[:, cols], ALU.mult, ALU.add)
             nc.sync.dma_start(out=out[:, cols], in_=result[:])

from contextlib import ExitStack

import concourse.mybir as mybir

F32 = mybir.dt.float32
BF16 = mybir.dt.bfloat16
I32 = mybir.dt.int32
U32 = mybir.dt.uint32
U16 = mybir.dt.uint16
U8 = mybir.dt.uint8
FP8X4 = mybir.dt.float8_e4m3fn_x4
ALU = mybir.AluOpType
ACT = mybir.ActivationFunctionType

P = 128
PACK = 4
FEATURES = 512
TOKENS = 2048
SLOTS = 512
ROWS = 128
HALF = SLOTS // 2
OUT_WIDTHS = (576, 512, 448, 320, 192)

FLOPS = 2 * 2 * FEATURES * ROWS * SLOTS


def load_scales(nc, window, scales):
    nc.sync.dma_start(out=window[0:P:8, :].bitcast(I32), in_=scales[0].bitcast(I32))


def place_scales(nc, plane, gathered):
    nc.vector.tensor_copy(plane[:].bitcast(I32), gathered[:].bitcast(I32))
    for row in range(1, 4):
        nc.scalar.dma_start(out=plane[row:P:32, :].bitcast(I32), in_=gathered[8 * row : P : 32, :].bitcast(I32))


def load_words(nc, window, words):
    nc.sync.dma_start(out=window[:].bitcast(I32), in_=words[0].rearrange("p n t -> p (n t)").bitcast(I32))


def interleave(nc, grouped, raw):
    nc.scalar.copy(
        out=grouped[:].rearrange("p (c i) t -> p c t i", i=4),
        in_=raw[:].rearrange("p t (c i) -> p c t i", i=4),
    )


def quantize(nc, codes, plane, grouped):
    nc.vector.quantize_mx(out=codes[:].bitcast(FP8X4), scales=plane[:], in_=grouped[:].rearrange("p w t -> p (w t)"))


def tile_attend_bsquareshares_s_kernel(
    tc, query, keys_words, keys_scales, floor, reserve, gout, vals_words, vals_scales, old, offs, out
):
    nc = tc.nc
    with ExitStack() as ctx:
        sb = ctx.enter_context(tc.tile_pool(name="sb", bufs=1))
        psum = ctx.enter_context(tc.psum_pool(name="psum", bufs=1))

        offsets = sb.tile([P, SLOTS // 16], U16, name="offsets")
        key_words = sb.tile([P, TOKENS], U32, name="key_words", tag="keys_then_old")
        val_words = sb.tile([P, TOKENS], U32, name="val_words")
        key_plane = sb.tile([P, TOKENS], U8, name="key_plane")
        val_plane = sb.tile([P, TOKENS], U8, name="val_plane")
        placed = sb.tile([P, TOKENS], F32, name="placed")
        query_raw = sb.tile([P, PACK, ROWS], F32, name="query_raw", tag="query_then_plane", align_bytes=64)
        gout_raw = sb.tile([P, PACK, ROWS], F32, name="gout_raw", tag="gout_then_plane", align_bytes=64)
        floor_col = sb.tile([P, 1], F32, name="floor_col")
        reserve_col = sb.tile([P, 1], F32, name="reserve_col")

        nc.gpsimd.memset(key_plane[:, : TOKENS // 2].bitcast(I32), 0)
        nc.vector.memset(key_plane[:, TOKENS // 2 :].bitcast(I32), 0)
        nc.vector.memset(val_plane[:].bitcast(I32), 0)
        nc.vector.memset(placed[:], 0.0)

        nc.sync.dma_start(offsets[:], offs)
        nc.sync.dma_start(out=floor_col[:], in_=floor)
        nc.sync.dma_start(out=reserve_col[:], in_=reserve)
        nc.sync.dma_start(out=query_raw[:], in_=query.rearrange("(p t) w -> p t w", t=PACK))
        load_scales(nc, key_plane, keys_scales)
        nc.sync.dma_start(out=gout_raw[:], in_=gout.rearrange("(p t) w -> p t w", t=PACK))
        load_scales(nc, val_plane, vals_scales)
        load_words(nc, key_words, keys_words)
        load_words(nc, val_words, vals_words)

        query_bf = sb.tile([P, ROWS, PACK], BF16, name="query_bf", align_bytes=64)
        query_codes = sb.tile([P, ROWS], U32, name="query_codes", align_bytes=64)
        query_plane = sb.tile([P, ROWS], U8, name="query_plane", align_bytes=64)
        gout_bf = sb.tile([P, ROWS, PACK], BF16, name="gout_bf", align_bytes=64)
        gout_codes = sb.tile([P, ROWS], U32, name="gout_codes", align_bytes=64)
        gout_plane = sb.tile([P, ROWS], U8, name="gout_plane", align_bytes=64)
        interleave(nc, query_bf, query_raw)
        interleave(nc, gout_bf, gout_raw)

        key_rows_g = sb.tile([P, SLOTS], U8, name="key_rows_g")
        key_scales_g = sb.tile([P, SLOTS], U8, name="key_scales_g", tag="query_then_plane", align_bytes=64)
        nc.vector.tensor_copy(key_rows_g[:], key_plane[:].indirect(offsets[:]))
        place_scales(nc, key_scales_g, key_rows_g)
        val_rows_g = sb.tile([P, SLOTS], U8, name="val_rows_g")
        val_scales_g = sb.tile([P, SLOTS], U8, name="val_scales_g", tag="gout_then_plane", align_bytes=64)
        nc.vector.tensor_copy(val_rows_g[:], val_plane[:].indirect(offsets[:]))
        place_scales(nc, val_scales_g, val_rows_g)

        quantize(nc, query_codes, query_plane, query_bf)
        quantize(nc, gout_codes, gout_plane, gout_bf)
        key_words_g = sb.tile([P, SLOTS], U32, name="key_words_g", align_bytes=64)
        nc.vector.tensor_copy(key_words_g[:], key_words[:].indirect(offsets[:]))

        old_sb = sb.tile([P, TOKENS], F32, name="old_sb", tag="keys_then_old")
        nc.sync.dma_start(out=old_sb[:], in_=old)

        a_ps = psum.tile([P, SLOTS], F32, name="a_ps")
        nc.tensor.matmul_mx(
            out=a_ps[:],
            lhsT=query_codes[:].bitcast(FP8X4),
            lhsT_scale=query_plane[:],
            rhs=key_words_g[:].bitcast(FP8X4),
            rhs_scale=key_scales_g[:],
            start=True,
            stop=True,
        )

        a_sq = sb.tile([P, SLOTS], F32, name="a_sq")
        sum_sq = sb.tile([P, 1], F32, name="sum_sq")
        base = sb.tile([P, 1], F32, name="base")
        z = sb.tile([P, 1], F32, name="z")
        nc.scalar.activation(a_sq[:], a_ps[:], ACT.Square, accum_out=sum_sq[:])
        nc.gpsimd.tensor_scalar(base[:], floor_col[:], float(SLOTS), reserve_col[:], ALU.mult, ALU.add)
        nc.scalar.activation(z[:], sum_sq[:], ACT.Identity, bias=base[:])

        c_ps = []
        for h in range(2):
            val_words_g = sb.tile([P, HALF], U32, name="val_words_g%d" % h, align_bytes=64)
            nc.vector.tensor_copy(val_words_g[:], val_words[:].indirect(offsets[:, 16 * h : 16 * (h + 1)]))
            bank = psum.tile([P, HALF], F32, name="c_ps%d" % h)
            nc.tensor.matmul_mx(
                out=bank[:],
                lhsT=gout_codes[:].bitcast(FP8X4),
                lhsT_scale=gout_plane[:],
                rhs=val_words_g[:].bitcast(FP8X4),
                rhs_scale=val_scales_g[:, HALF * h : HALF * (h + 1)],
                start=True,
                stop=True,
            )
            c_ps.append(bank)

        a_sb = sb.tile([P, SLOTS], F32, name="a_sb")
        nc.scalar.copy(a_sb[:], a_ps[:])

        def weighted_sum(h):
            cp = sb.tile([P, HALF], F32, name="cp%d" % h)
            cp_sum = sb.tile([P, 1], F32, name="cp_sum%d" % h)
            nc.vector.scalar_tensor_tensor(
                cp[:], a_sq[:, HALF * h : HALF * (h + 1)], floor_col[:], c_ps[h][:], ALU.add, ALU.mult, accum_out=cp_sum[:]
            )
            return cp_sum

        def scatter(h, t_half):
            nc.vector.tensor_tensor(
                placed[:].indirect(offsets[:, 16 * h : 16 * (h + 1)]), a_sb[:, HALF * h : HALF * (h + 1)], t_half[:], ALU.mult
            )

        sum_first = weighted_sum(0)
        cz_first = sb.tile([P, HALF], F32, name="cz_first")
        nc.scalar.activation(cz_first[:], c_ps[0][:], ACT.Copy, scale=z[:])
        sum_second = weighted_sum(1)

        t_first = sb.tile([P, HALF], F32, name="t_first", tag="t_first_then_inv_z")
        nc.vector.tensor_scalar(t_first[:], cz_first[:], sum_first[:], sum_second[:], ALU.subtract, ALU.subtract)
        scatter(0, t_first)

        cp_total = sb.tile([P, 1], F32, name="cp_total")
        neg_cp_total = sb.tile([P, 1], F32, name="neg_cp_total")
        t_second = sb.tile([P, HALF], F32, name="t_second")
        nc.scalar.activation(cp_total[:], sum_first[:], ACT.Identity, bias=sum_second[:])
        nc.scalar.activation(neg_cp_total[:], cp_total[:], ACT.Copy, scale=-1.0)
        nc.scalar.activation(t_second[:], c_ps[1][:], ACT.Identity, scale=z[:], bias=neg_cp_total[:])
        inv_z = sb.tile([P, 1], F32, name="inv_z", tag="t_first_then_inv_z")
        row_factor = sb.tile([P, 1], F32, name="row_factor")
        nc.vector.reciprocal(inv_z[:], z[:])
        nc.scalar.activation(row_factor[:], inv_z[:], ACT.Square, scale=32.0)
        scatter(1, t_second)

        first = 0
        for c, width in enumerate(OUT_WIDTHS):
            cols = slice(first, first + width)
            first = first + width
            result = sb.tile([P, width], F32, name="result%d" % c)
            nc.vector.scalar_tensor_tensor(result[:], placed[:, cols], row_factor[:], old_sb[:, cols], ALU.mult, ALU.add)
            nc.sync.dma_start(out=out[:, cols], in_=result[:])
